import numpy as np, ml_dtypes
CORES = [23,119,17,113]
N = 4
import mx_ref
NC, KT, ROOT = 128, 2, 3
BF = ml_dtypes.bfloat16
def setup_inputs(rng):
    def f(*shape):
        return mx_ref.flush((rng.standard_normal(shape, dtype=np.float32) * np.exp2(rng.integers(-2, 3, shape[:-1] + (1,)))).astype(BF))
    return {"w": f(N, 128, KT * 512), "x": f(N, 128, N * KT * 4 * NC)}
def setup_inputs_blocks(rng):
    d = setup_inputs(rng)
    for k in ("w", "x"): d[k] = mx_ref.spread(d[k], rng, 4)
    return d
def setup_inputs_wide(rng):
    d = setup_inputs(rng)
    for k in ("w", "x"): d[k] = mx_ref.flush((d[k].astype(np.float32) * np.exp2(rng.integers(-8, 9, (N, 1, 1))).astype(np.float32)).astype(BF))
    return d
def setup_inputs_zeros(rng):
    d = setup_inputs(rng); v = d["x"].reshape(N, 128, -1, 4).copy()
    v[np.broadcast_to((rng.random((N, 1, v.shape[2], 1)) < 0.33), v.shape)] = 0
    d["x"] = v.reshape(d["x"].shape)
    return d
def reference(w, x):
    y = np.zeros((N, 128, NC), np.float32)
    for r in range(N):
        for t in range(KT):
            p = mx_ref.matmul(mx_ref.quantize(w[r][:, 512 * t:512 * t + 512]), mx_ref.quantize(x[ROOT][:, 4 * NC * (KT * r + t):4 * NC * (KT * r + t) + 4 * NC]))
            y[r] = p if t == 0 else y[r] + p
    return {"y": y}

from concourse.bass import DstId, RemoteDMATransfer
from concourse.mybir import dt

KT = 2
NC = 128
RW = KT * NC
NR = 4

SCRATCH = {
    "xb": ("sbuf", [128, NR * RW * 4], "bfloat16"),
    "xq": ("sbuf", [128, NR * RW], "float8_e4m3fn_x4"),
    "xs": ("sbuf", [128, NR * RW], "uint8"),
    "wb": ("sbuf", [128, RW * 4], "bfloat16"),
    "wq": ("sbuf", [128, RW], "float8_e4m3fn_x4"),
    "ws": ("sbuf", [128, RW], "uint8"),
    "lq": ("sbuf", [128, RW], "float8_e4m3fn_x4"),
    "ls": ("sbuf", [128, RW], "uint8"),
    "ps": ("psum", [128, 512], "float32"),
    "yb": ("sbuf", [128, NC], "float32"),
}
SEMAPHORES = ["ld0", "ld1", "ld2", "ld3", "ldw", "q0", "q1", "q2", "q3", "qw",
              "arrived", "sent", "mm", "cp", "st"]


def _bits(mask):
    return [1 << i for i in range(mask.bit_length()) if (mask >> i) & 1]


def _join(bits):
    m = 0
    for b in bits:
        m |= b
    return m


def _plan(T, topo):
    root = T.cores[T.root]
    others = [r for r in range(len(T.cores)) if r != T.root]
    far = [r for r in others if topo.chip(T.cores[r]) != topo.chip(root)]
    near = [r for r in others if topo.chip(T.cores[r]) == topo.chip(root)]
    far.sort(key=lambda r: topo.die(T.cores[r]) == topo.die(root))
    out = _bits(topo.mask(root, T.cores[far[0]]))
    stay = [b for b in _bits(topo.mask(root, T.cores[near[0]])) if b not in out]
    half = len(out) // 2
    calls = [
        [(far[0], "q", _join(out))],
        [(far[1], "q", _join(out)), (near[0], "q", _join(stay))],
        [(far[0], "s", _join(out[:half])), (far[1], "s", _join(out[half:])), (near[0], "s", _join(stay))],
    ]
    return far + near, calls


def _load(g, buf, src, a, b, sem):
    g.sync.dma_start(buf[0:64, a:b], src[0:64, a:b]).then_inc(sem, 16)
    g.scalar.dma_start(buf[64:128, a:b], src[64:128, a:b]).then_inc(sem, 16)


def rank_program(g, core, T, topo):
    rank = T.rank_of(core)
    if rank is None:
        return
    order, calls = _plan(T, topo)
    is_root = rank == T.root

    if is_root:
        for r in order:
            _load(g, T.xb, T.x, 4 * RW * r, 4 * RW * (r + 1), T.sem["ld%d" % r])
    _load(g, T.wb, T.w, 0, 4 * RW, T.sem.ldw)
    if is_root:
        _load(g, T.xb, T.x, 4 * RW * rank, 4 * RW * (rank + 1), T.sem["ld%d" % rank])

    def quant_x(r):
        g.vector.wait_ge(T.sem["ld%d" % r], 32)
        g.vector.quantize_mx(T.xq[:, RW * r:RW * (r + 1)], T.xs[:, RW * r:RW * (r + 1)],
                             T.xb[:, 4 * RW * r:4 * RW * (r + 1)]).then_inc(T.sem["q%d" % r], 1)

    if is_root:
        for r in order:
            quant_x(r)
    g.vector.wait_ge(T.sem.ldw, 32)
    g.vector.quantize_mx(T.wq[:], T.ws[:], T.wb[:]).then_inc(T.sem.qw, 1)
    if is_root:
        quant_x(rank)

    if is_root:
        seen = []
        left = 0
        for call in calls:
            trs = []
            for (r, kind, mask) in call:
                if r not in seen:
                    g.wait_ge(T.sem["q%d" % r], 1)
                    seen.append(r)
                rid, pid, _se = topo.addr(T.cores[r])
                if kind == "q":
                    src, dst = T.xq[:, RW * r:RW * (r + 1)].bitcast(dt.uint8), T.lq[:].bitcast(dt.uint8)
                else:
                    src, dst = T.xs[:, RW * r:RW * (r + 1)], T.ls[:]
                trs.append(RemoteDMATransfer(dst_ids=[DstId(rid=rid, pnc=pid)], dma_engine_mask=mask,
                                             remote_sem=T.sem.arrived, src=src, dst=dst))
                left += len(_bits(mask))
            g.remote_dma_fused(trs, local_sem=T.sem.sent)
        g.wait_ge(T.sem.sent, left)

    g.tensor.wait_ge(T.sem.qw, 1)
    if is_root:
        g.tensor.wait_ge(T.sem["q%d" % rank], 1)
        xq, xs, base = T.xq, T.xs, RW * rank
    else:
        due = sum(len(_bits(m)) for call in calls for (r, _k, m) in call if r == rank)
        g.tensor.wait_ge(T.sem.arrived, due)
        xq, xs, base = T.lq, T.ls, 0
    for t in range(KT):
        mm = g.tensor.matmul_mx(T.ps[:, 0:NC], T.wq[:, NC * t:NC * (t + 1)], T.ws[:, NC * t:NC * (t + 1)],
                                xq[:, base + NC * t:base + NC * (t + 1)], xs[:, base + NC * t:base + NC * (t + 1)],
                                t == 0, t == KT - 1)
    mm.then_inc(T.sem.mm, 1)

    g.vector.wait_ge(T.sem.mm, 1)
    g.vector.tensor_copy(T.yb[:], T.ps[:, 0:NC]).then_inc(T.sem.cp, 1)
    g.sync.wait_ge(T.sem.cp, 1)
    g.sync.dma_start(T.y[:, :], T.yb[:, :]).then_inc(T.sem.st, 16)
    g.sync.wait_ge(T.sem.st, 16)
